import numpy as np
import ml_dtypes


def mxq(x, axis, fmt="e4m3"):
    dtype, down = {"e4m3": (ml_dtypes.float8_e4m3fn, 7), "e5m2": (ml_dtypes.float8_e5m2, 14)}[fmt]
    v = np.moveaxis(np.asarray(x, np.float32).astype(ml_dtypes.bfloat16).astype(np.float64), axis, -1)
    blocks = v.reshape(v.shape[:-1] + (-1, 32))
    amax = np.abs(blocks).max(-1, keepdims=True)
    byte = np.maximum(np.where(amax > 0, np.frexp(amax)[1] - 1 + 127, 0) - down, 1)
    scale = np.exp2(byte - 127.0)
    codes = (blocks / scale).astype(np.float32).astype(dtype).astype(np.float64)
    return np.moveaxis((codes * scale).reshape(v.shape), -1, axis)


WIDE = False


def mx_kscale(k):
    if not WIDE:
        return np.ones(k)
    levels = np.array([10, -10, 5, -5, 0])
    if k % 512:
        return np.exp2(np.random.permutation(np.resize(levels, k // 32))).repeat(32)
    a = np.empty((k // 512, 16))
    for p in range(k // 512):
        a[p, :8] = np.random.permutation(np.resize(levels, 8))
        for g in range(8):
            far = levels[np.abs(levels - a[p, g]) >= 10]
            a[p, g + 8] = far[np.random.randint(len(far))]
    return np.exp2(a.ravel()).repeat(32)


def f64(x):
    return np.asarray(x).astype(np.float64)


E2M1 = np.array([0.0, 0.5, 1.0, 1.5, 2.0, 3.0, 4.0, 6.0, -0.0, -0.5, -1.0, -1.5, -2.0, -3.0, -4.0, -6.0])


def pack_weight(w, fmt):
    k, n = w.shape
    w = f64(np.asarray(w, np.float32).astype(ml_dtypes.bfloat16)).reshape(k // 32, 32, n)
    amax = np.abs(w).max(1)
    if fmt == "e4m3":
        byte = np.frexp(amax)[1] - 1 + 127 - 7
    else:
        mant, ex = np.frexp(amax / 6.0)
        byte = np.where(mant > 0.5, ex, ex - 1) + 127
    byte = np.clip(np.where(amax > 0, byte, 1), 1, 254)
    scaled = (w * np.exp2(127.0 - byte)[:, None, :]).reshape(k, n).astype(np.float32)
    by_word = np.ascontiguousarray(scaled.reshape(k // 512, 128, 4, n).transpose(0, 1, 3, 2))
    if fmt == "e4m3":
        words = by_word.astype(ml_dtypes.float8_e4m3fn).view(np.uint8)
    else:
        c = by_word.astype(ml_dtypes.float4_e2m1fn).view(np.uint8) & 0xF
        words = (c[..., 0::2] | (c[..., 1::2] << 4)).reshape(k // 512, 128, 2 * n)
    return np.ascontiguousarray(words), np.ascontiguousarray(byte.astype(np.uint8).reshape(k // 512, 16, n))


def unpack_weight(words, scales, fmt):
    g, _, n = scales.shape
    words = np.ascontiguousarray(words).reshape(g, 128, n, -1)
    if fmt == "e4m3":
        vals = words.view(ml_dtypes.float8_e4m3fn).astype(np.float64)
    else:
        nib = np.empty((g, 128, n, 4), np.uint8)
        nib[..., 0::2] = words & 0xF
        nib[..., 1::2] = words >> 4
        vals = E2M1[nib]
    vals = vals * np.repeat(np.exp2(scales.astype(np.float64) - 127.0), 8, axis=1)[..., None]
    return vals.transpose(0, 1, 3, 2).reshape(g * 512, n)


K, M, T = 1024, 1536, 512


def setup_inputs():
    n = np.random.standard_normal
    s = mx_kscale(K)[:, None]
    w = n((K, M)) / np.sqrt(K) / s
    w4 = pack_weight(w, "e2m1")
    rest = w - unpack_weight(*w4, "e2m1")
    p_r8 = pack_weight(rest, "e4m3")
    return {
        "x": (n((K, T)) * s).astype(np.float32),
        "w4_words": w4[0],
        "w4_scales": w4[1],
        "r8_words": p_r8[0],
        "r8_scales": p_r8[1],
    }


def reference(x, w4_words, w4_scales, r8_words, r8_scales):
    x_ = mxq(f64(x), 0, "e4m3")
    w4_ = unpack_weight(w4_words, w4_scales, "e2m1")
    r8_ = unpack_weight(r8_words, r8_scales, "e4m3")
    y = w4_.T @ x_ + r8_.T @ x_
    return np.maximum(y, 0.0) ** 2

@@ -1,0 +1,172 @@
+from contextlib import ExitStack
+
+import concourse.mybir as mybir
+
+K, N_OUT, T = 1024, 1536, 512
+FLOPS = 2 * (2 * K * N_OUT * T)
+
+F32 = mybir.dt.float32
+BF16 = mybir.dt.bfloat16
+I32 = mybir.dt.int32
+U32 = mybir.dt.uint32
+U8 = mybir.dt.uint8
+E4M3 = mybir.dt.float8_e4m3fn_x4
+E2M1 = mybir.dt.float4_e2m1fn_x4
+ACT = mybir.ActivationFunctionType
+ALU = mybir.AluOpType
+
+P = 128
+PACK = 4
+K_PASS = P * PACK
+PASSES = K // K_PASS
+CHUNK = 256
+VEC_COLS = 160
+BANKS = 8
+
+
+def tile_mix_resid_fm_relu2_kernel(tc, x, w4_words, w4_scales, r8_words, r8_scales, out):
+    nc = tc.nc
+    n_tiles = N_OUT // P
+    first = BANKS * P
+
+    with ExitStack() as ctx:
+        keep = ctx.enter_context(tc.tile_pool(name="keep", bufs=1))
+        work = ctx.enter_context(tc.tile_pool(name="work", bufs=n_tiles))
+        psum = ctx.enter_context(tc.psum_pool(name="psum", bufs=1))
+        ctx.enter_context(tc.manual_schedule())
+
+        one = keep.tile([P, 1], F32, name="one")
+        r8_planes = keep.tile([P, N_OUT], U8, name="r8_planes", align_bytes=64)
+        w4_planes = keep.tile([P, PASSES, N_OUT], U8, name="w4_planes", align_bytes=64)
+        nc.vector.memset(one[:], 0.0)
+        nc.vector.memset(r8_planes[:].bitcast(I32), 0)
+        nc.vector.memset(w4_planes[:].rearrange("p a n -> p (a n)").bitcast(I32), 0)
+        nc.scalar.activation(out=one[:], in_=one[:], func=ACT.Relu)
+
+        x_codes = [keep.tile([P, T], U32, name="x_codes%d" % a, align_bytes=64) for a in range(PASSES)]
+        x_scales = [keep.tile([P, T], U8, name="x_scales%d" % a, align_bytes=64) for a in range(PASSES)]
+        x_raw = {}
+
+        def load_x(a, c):
+            raw = keep.tile([P, PACK, CHUNK], F32, name="x_raw%d_%d" % (a, c))
+            nc.sync.dma_start(
+                out=raw[:],
+                in_=x[a * K_PASS : (a + 1) * K_PASS, c : c + CHUNK].rearrange("(p j) w -> p j w", j=PACK),
+            )
+            x_raw[(a, c)] = raw
+
+        def quantize_x(a, c):
+            raw = x_raw[(a, c)]
+            grouped = keep.tile([P, CHUNK, PACK], BF16, name="x_grouped%d_%d" % (a, c), align_bytes=64)
+            nc.vector.tensor_copy(
+                out=grouped[:, 0:VEC_COLS, :], in_=raw[:, :, 0:VEC_COLS].rearrange("p j w -> p w j")
+            )
+            nc.scalar.copy(
+                out=grouped[:, VEC_COLS:CHUNK, :], in_=raw[:, :, VEC_COLS:CHUNK].rearrange("p j w -> p w j")
+            )
+            nc.vector.quantize_mx(
+                out=x_codes[a][:, c : c + CHUNK].bitcast(E4M3),
+                scales=x_scales[a][:, c : c + CHUNK],
+                in_=grouped[:].rearrange("p w j -> p (w j)"),
+            )
+
+        r8_parts = {}
+        w4_parts = {}
+
+        def load_r8(a, n0, n1):
+            words = keep.tile([P, n1 - n0], U32, name="r8_%d_%d" % (a, n0), align_bytes=64)
+            nc.sync.dma_start(
+                out=words[:].bitcast(I32),
+                in_=r8_words[a].rearrange("p n i -> p (n i)")[:, PACK * n0 : PACK * n1].bitcast(I32),
+            )
+            for m in range(n0 // P, n1 // P):
+                r8_parts[(a, m)] = words[:, m * P - n0 : (m + 1) * P - n0].bitcast(E4M3)
+
+        def load_w4(a, n0, n1):
+            words = keep.tile([P, 2 * (n1 - n0)], U8, name="w4_%d_%d" % (a, n0), align_bytes=64)
+            nc.sync.dma_start(out=words[:].bitcast(I32), in_=w4_words[a][:, 2 * n0 : 2 * n1].bitcast(I32))
+            for m in range(n0 // P, n1 // P):
+                w4_parts[(a, m)] = words[:, 2 * (m * P - n0) : 2 * ((m + 1) * P - n0)].bitcast(E2M1)
+
+        load_x(0, 0)
+        load_x(0, CHUNK)
+        for q in range(4):
+            nc.sync.dma_start(
+                out=r8_planes[32 * q + 4 : 32 * q + 12, :].bitcast(I32),
+                in_=r8_scales[:, 4 * q : 4 * q + 4, :].bitcast(I32),
+            )
+        load_r8(0, 0, first // 2)
+        load_r8(0, first // 2, first)
+        for q in range(4):
+            nc.sync.dma_start(
+                out=w4_planes[32 * q : 32 * q + 4, :, :].bitcast(I32),
+                in_=w4_scales[:, 4 * q : 4 * q + 4, :].rearrange("a q n -> q a n").bitcast(I32),
+            )
+        load_w4(0, 0, first)
+        load_x(1, 0)
+        load_x(1, CHUNK)
+        load_r8(1, 0, first)
+        load_w4(1, 0, first)
+        load_r8(0, first, N_OUT)
+        load_w4(0, first, N_OUT)
+        load_r8(1, first, N_OUT)
+        load_w4(1, first, N_OUT)
+
+        for a in range(PASSES):
+            for c in range(0, T, CHUNK):
+                quantize_x(a, c)
+
+        acc = {}
+
+        def open_bank(m):
+            bank = psum.tile([P, T], F32, name="bank%d" % (m % BANKS))
+            acc[m] = bank
+
+        def add_r8(m, a, start=False):
+            nc.tensor.matmul_mx(
+                out=acc[m][:],
+                lhsT=r8_parts[(a, m)],
+                lhsT_scale=r8_planes[4 + 4 * a :, m * P : (m + 1) * P],
+                rhs=x_codes[a][:].bitcast(E4M3),
+                rhs_scale=x_scales[a][:],
+                start=start,
+                stop=False,
+            )
+
+        def add_w4(m, a, stop=False):
+            nc.tensor.matmul_mx(
+                out=acc[m][:],
+                lhsT=w4_parts[(a, m)],
+                lhsT_scale=w4_planes[:, a, m * P : (m + 1) * P],
+                rhs=x_codes[a][:].bitcast(E4M3),
+                rhs_scale=x_scales[a][:],
+                start=False,
+                stop=stop,
+            )
+
+        def finish(m, pieces):
+            relu = work.tile([P, T], F32, name="relu")
+            result = work.tile([P, T], F32, name="result")
+            width = T // pieces
+            for c in range(0, T, width):
+                cols = slice(c, c + width)
+                nc.scalar.activation(out=relu[:, cols], in_=acc[m][:, cols], func=ACT.Relu)
+                nc.vector.tensor_tensor(out=result[:, cols], in0=relu[:, cols], in1=relu[:, cols], op=ALU.mult)
+                nc.sync.dma_start(out=out[m * P : (m + 1) * P, cols], in_=result[:, cols])
+
+        for m in range(BANKS):
+            open_bank(m)
+            add_r8(m, 0, start=True)
+        for m in range(BANKS):
+            add_w4(m, 0)
+        for m in range(BANKS):
+            add_r8(m, 1)
+            add_w4(m, 1, stop=True)
+            finish(m, 1)
+        for m in range(BANKS, n_tiles):
+            open_bank(m)
+            add_r8(m, 0, start=True)
+            add_w4(m, 0)
+            add_r8(m, 1)
+            add_w4(m, 1, stop=True)
+            finish(m, 2 if m == n_tiles - 1 else 1)

@@ -38,9 +38,19 @@ def tile_mix_resid_fm_relu2_kernel(tc, x, w4_words, w4_scales, r8_words, r8_scal
         one = keep.tile([P, 1], F32, name="one")
         r8_planes = keep.tile([P, N_OUT], U8, name="r8_planes", align_bytes=64)
         w4_planes = keep.tile([P, PASSES, N_OUT], U8, name="w4_planes", align_bytes=64)
-        nc.vector.memset(one[:], 0.0)
+        nc.gpsimd.memset(one[:], 0.0)
         nc.vector.memset(r8_planes[:].bitcast(I32), 0)
         nc.vector.memset(w4_planes[:].rearrange("p a n -> p (a n)").bitcast(I32), 0)
+        for q in range(4):
+            nc.scalar.dma_start(
+                out=r8_planes[32 * q + 4 : 32 * q + 12, :].bitcast(I32),
+                in_=r8_scales[:, 4 * q : 4 * q + 4, :].bitcast(I32),
+            )
+        for q in range(4):
+            nc.gpsimd.dma_start(
+                out=w4_planes[32 * q : 32 * q + 4, :, :].bitcast(I32),
+                in_=w4_scales[:, 4 * q : 4 * q + 4, :].rearrange("a q n -> q a n").bitcast(I32),
+            )
         nc.scalar.activation(out=one[:], in_=one[:], func=ACT.Relu)
 
         x_codes = [keep.tile([P, T], U32, name="x_codes%d" % a, align_bytes=64) for a in range(PASSES)]
@@ -90,18 +100,8 @@ def tile_mix_resid_fm_relu2_kernel(tc, x, w4_words, w4_scales, r8_words, r8_scal
 
         load_x(0, 0)
         load_x(0, CHUNK)
-        for q in range(4):
-            nc.sync.dma_start(
-                out=r8_planes[32 * q + 4 : 32 * q + 12, :].bitcast(I32),
-                in_=r8_scales[:, 4 * q : 4 * q + 4, :].bitcast(I32),
-            )
         load_r8(0, 0, first // 2)
         load_r8(0, first // 2, first)
-        for q in range(4):
-            nc.sync.dma_start(
-                out=w4_planes[32 * q : 32 * q + 4, :, :].bitcast(I32),
-                in_=w4_scales[:, 4 * q : 4 * q + 4, :].rearrange("a q n -> q a n").bitcast(I32),
-            )
         load_w4(0, 0, first)
         load_x(1, 0)
         load_x(1, CHUNK)

from contextlib import ExitStack

import concourse.mybir as mybir

K, N_OUT, T = 1024, 1536, 512
FLOPS = 2 * (2 * K * N_OUT * T)

F32 = mybir.dt.float32
BF16 = mybir.dt.bfloat16
I32 = mybir.dt.int32
U32 = mybir.dt.uint32
U8 = mybir.dt.uint8
E4M3 = mybir.dt.float8_e4m3fn_x4
E2M1 = mybir.dt.float4_e2m1fn_x4
ACT = mybir.ActivationFunctionType
ALU = mybir.AluOpType

P = 128
PACK = 4
K_PASS = P * PACK
PASSES = K // K_PASS
CHUNK = 256
VEC_COLS = 160
BANKS = 8


def tile_mix_resid_fm_relu2_kernel(tc, x, w4_words, w4_scales, r8_words, r8_scales, out):
    nc = tc.nc
    n_tiles = N_OUT // P
    first = BANKS * P

    with ExitStack() as ctx:
        keep = ctx.enter_context(tc.tile_pool(name="keep", bufs=1))
        work = ctx.enter_context(tc.tile_pool(name="work", bufs=n_tiles))
        psum = ctx.enter_context(tc.psum_pool(name="psum", bufs=1))
        ctx.enter_context(tc.manual_schedule())

        one = keep.tile([P, 1], F32, name="one")
        r8_planes = keep.tile([P, N_OUT], U8, name="r8_planes", align_bytes=64)
        w4_planes = keep.tile([P, PASSES, N_OUT], U8, name="w4_planes", align_bytes=64)
        nc.gpsimd.memset(one[:], 0.0)
        nc.vector.memset(r8_planes[:].bitcast(I32), 0)
        nc.vector.memset(w4_planes[:].rearrange("p a n -> p (a n)").bitcast(I32), 0)
        for q in range(4):
            nc.scalar.dma_start(
                out=r8_planes[32 * q + 4 : 32 * q + 12, :].bitcast(I32),
                in_=r8_scales[:, 4 * q : 4 * q + 4, :].bitcast(I32),
            )
        for q in range(4):
            nc.gpsimd.dma_start(
                out=w4_planes[32 * q : 32 * q + 4, :, :].bitcast(I32),
                in_=w4_scales[:, 4 * q : 4 * q + 4, :].rearrange("a q n -> q a n").bitcast(I32),
            )
        nc.scalar.activation(out=one[:], in_=one[:], func=ACT.Relu)

        x_codes = [keep.tile([P, T], U32, name="x_codes%d" % a, align_bytes=64) for a in range(PASSES)]
        x_scales = [keep.tile([P, T], U8, name="x_scales%d" % a, align_bytes=64) for a in range(PASSES)]
        x_raw = {}

        def load_x(a, c):
            raw = keep.tile([P, PACK, CHUNK], F32, name="x_raw%d_%d" % (a, c))
            nc.sync.dma_start(
                out=raw[:],
                in_=x[a * K_PASS : (a + 1) * K_PASS, c : c + CHUNK].rearrange("(p j) w -> p j w", j=PACK),
            )
            x_raw[(a, c)] = raw

        def quantize_x(a, c):
            raw = x_raw[(a, c)]
            grouped = keep.tile([P, CHUNK, PACK], BF16, name="x_grouped%d_%d" % (a, c), align_bytes=64)
            nc.vector.tensor_copy(
                out=grouped[:, 0:VEC_COLS, :], in_=raw[:, :, 0:VEC_COLS].rearrange("p j w -> p w j")
            )
            nc.scalar.copy(
                out=grouped[:, VEC_COLS:CHUNK, :], in_=raw[:, :, VEC_COLS:CHUNK].rearrange("p j w -> p w j")
            )
            nc.vector.quantize_mx(
                out=x_codes[a][:, c : c + CHUNK].bitcast(E4M3),
                scales=x_scales[a][:, c : c + CHUNK],
                in_=grouped[:].rearrange("p w j -> p (w j)"),
            )

        r8_parts = {}
        w4_parts = {}

        def load_r8(a, n0, n1):
            words = keep.tile([P, n1 - n0], U32, name="r8_%d_%d" % (a, n0), align_bytes=64)
            nc.sync.dma_start(
                out=words[:].bitcast(I32),
                in_=r8_words[a].rearrange("p n i -> p (n i)")[:, PACK * n0 : PACK * n1].bitcast(I32),
            )
            for m in range(n0 // P, n1 // P):
                r8_parts[(a, m)] = words[:, m * P - n0 : (m + 1) * P - n0].bitcast(E4M3)

        def load_w4(a, n0, n1):
            words = keep.tile([P, 2 * (n1 - n0)], U8, name="w4_%d_%d" % (a, n0), align_bytes=64)
            nc.sync.dma_start(out=words[:].bitcast(I32), in_=w4_words[a][:, 2 * n0 : 2 * n1].bitcast(I32))
            for m in range(n0 // P, n1 // P):
                w4_parts[(a, m)] = words[:, 2 * (m * P - n0) : 2 * ((m + 1) * P - n0)].bitcast(E2M1)

        load_x(0, 0)
        load_x(0, CHUNK)
        load_r8(0, 0, first // 2)
        load_r8(0, first // 2, first)
        load_w4(0, 0, first)
        load_x(1, 0)
        load_x(1, CHUNK)
        load_r8(1, 0, first)
        load_w4(1, 0, first)
        load_r8(0, first, N_OUT)
        load_w4(0, first, N_OUT)
        load_r8(1, first, N_OUT)
        load_w4(1, first, N_OUT)

        for a in range(PASSES):
            for c in range(0, T, CHUNK):
                quantize_x(a, c)

        acc = {}

        def open_bank(m):
            bank = psum.tile([P, T], F32, name="bank%d" % (m % BANKS))
            acc[m] = bank

        def add_r8(m, a, start=False):
            nc.tensor.matmul_mx(
                out=acc[m][:],
                lhsT=r8_parts[(a, m)],
                lhsT_scale=r8_planes[4 + 4 * a :, m * P : (m + 1) * P],
                rhs=x_codes[a][:].bitcast(E4M3),
                rhs_scale=x_scales[a][:],
                start=start,
                stop=False,
            )

        def add_w4(m, a, stop=False):
            nc.tensor.matmul_mx(
                out=acc[m][:],
                lhsT=w4_parts[(a, m)],
                lhsT_scale=w4_planes[:, a, m * P : (m + 1) * P],
                rhs=x_codes[a][:].bitcast(E4M3),
                rhs_scale=x_scales[a][:],
                start=False,
                stop=stop,
            )

        def finish(m, pieces):
            relu = work.tile([P, T], F32, name="relu")
            result = work.tile([P, T], F32, name="result")
            width = T // pieces
            for c in range(0, T, width):
                cols = slice(c, c + width)
                nc.scalar.activation(out=relu[:, cols], in_=acc[m][:, cols], func=ACT.Relu)
                nc.vector.tensor_tensor(out=result[:, cols], in0=relu[:, cols], in1=relu[:, cols], op=ALU.mult)
                nc.sync.dma_start(out=out[m * P : (m + 1) * P, cols], in_=result[:, cols])

        for m in range(BANKS):
            open_bank(m)
            add_r8(m, 0, start=True)
        for m in range(BANKS):
            add_w4(m, 0)
        for m in range(BANKS):
            add_r8(m, 1)
            add_w4(m, 1, stop=True)
            finish(m, 1)
        for m in range(BANKS, n_tiles):
            open_bank(m)
            add_r8(m, 0, start=True)
            add_w4(m, 0)
            add_r8(m, 1)
            add_w4(m, 1, stop=True)
            finish(m, 2 if m == n_tiles - 1 else 1)
